import numpy as np
import ml_dtypes


def mxq(x, axis, fmt="e4m3"):
    dtype, down = {"e4m3": (ml_dtypes.float8_e4m3fn, 7), "e5m2": (ml_dtypes.float8_e5m2, 14)}[fmt]
    v = np.moveaxis(np.asarray(x, np.float32).astype(ml_dtypes.bfloat16).astype(np.float64), axis, -1)
    blocks = v.reshape(v.shape[:-1] + (-1, 32))
    amax = np.abs(blocks).max(-1, keepdims=True)
    byte = np.maximum(np.where(amax > 0, np.frexp(amax)[1] - 1 + 127, 0) - down, 1)
    scale = np.exp2(byte - 127.0)
    codes = (blocks / scale).astype(np.float32).astype(dtype).astype(np.float64)
    return np.moveaxis((codes * scale).reshape(v.shape), -1, axis)


WIDE = False


def mx_kscale(k):
    if not WIDE:
        return np.ones(k)
    levels = np.array([10, -10, 5, -5, 0])
    if k % 512:
        return np.exp2(np.random.permutation(np.resize(levels, k // 32))).repeat(32)
    a = np.empty((k // 512, 16))
    for p in range(k // 512):
        a[p, :8] = np.random.permutation(np.resize(levels, 8))
        for g in range(8):
            far = levels[np.abs(levels - a[p, g]) >= 10]
            a[p, g + 8] = far[np.random.randint(len(far))]
    return np.exp2(a.ravel()).repeat(32)


def f64(x):
    return np.asarray(x).astype(np.float64)


def striped(idx):
    return np.tile(idx.reshape(-1, 16).T, (8, 1)).astype(np.uint16)


def unstriped(offs):
    return offs[:16].T.reshape(-1).astype(np.int64)


E2M1 = np.array([0.0, 0.5, 1.0, 1.5, 2.0, 3.0, 4.0, 6.0, -0.0, -0.5, -1.0, -1.5, -2.0, -3.0, -4.0, -6.0])


def pack_weight(w, fmt):
    k, n = w.shape
    w = f64(np.asarray(w, np.float32).astype(ml_dtypes.bfloat16)).reshape(k // 32, 32, n)
    amax = np.abs(w).max(1)
    if fmt == "e4m3":
        byte = np.frexp(amax)[1] - 1 + 127 - 7
    else:
        mant, ex = np.frexp(amax / 6.0)
        byte = np.where(mant > 0.5, ex, ex - 1) + 127
    byte = np.clip(np.where(amax > 0, byte, 1), 1, 254)
    scaled = (w * np.exp2(127.0 - byte)[:, None, :]).reshape(k, n).astype(np.float32)
    by_word = np.ascontiguousarray(scaled.reshape(k // 512, 128, 4, n).transpose(0, 1, 3, 2))
    if fmt == "e4m3":
        words = by_word.astype(ml_dtypes.float8_e4m3fn).view(np.uint8)
    else:
        c = by_word.astype(ml_dtypes.float4_e2m1fn).view(np.uint8) & 0xF
        words = (c[..., 0::2] | (c[..., 1::2] << 4)).reshape(k // 512, 128, 2 * n)
    return np.ascontiguousarray(words), np.ascontiguousarray(byte.astype(np.uint8).reshape(k // 512, 16, n))


def unpack_weight(words, scales, fmt):
    g, _, n = scales.shape
    words = np.ascontiguousarray(words).reshape(g, 128, n, -1)
    if fmt == "e4m3":
        vals = words.view(ml_dtypes.float8_e4m3fn).astype(np.float64)
    else:
        nib = np.empty((g, 128, n, 4), np.uint8)
        nib[..., 0::2] = words & 0xF
        nib[..., 1::2] = words >> 4
        vals = E2M1[nib]
    vals = vals * np.repeat(np.exp2(scales.astype(np.float64) - 127.0), 8, axis=1)[..., None]
    return vals.transpose(0, 1, 3, 2).reshape(g * 512, n)


def gelu(v):
    return 0.5 * v * (1.0 + np.tanh(np.sqrt(2.0 / np.pi) * (v + 0.044715 * v**3)))


K, T, S, H, N, T2 = 512, 4096, 1024, 1024, 512, 2048

def setup_inputs():
    n = np.random.standard_normal
    s = mx_kscale(K)[:, None]
    u = mx_kscale(H)[:, None]
    tab_words, tab_scales = pack_weight(n((K, T)) * s, "e4m3")
    wa = n((K, H)) / np.sqrt(K) / s
    wb_words, wb_scales = pack_weight(1.5 * n((K, H)) / np.sqrt(K) / s, "e2m1")
    gain = np.exp(0.3 * n(H)) * u[:, 0]
    wc = 3.0 * n((H, N)) / np.sqrt(H) / u
    return {
        "tab_words": tab_words, "tab_scales": tab_scales,
        "offs": striped(np.random.permutation(T)[:S]),
        "offs2": striped(np.random.permutation(T)[:S]),
        "offs3": striped(np.random.permutation(T2)[:S]),
        "wa": wa.astype(np.float32),
        "wb_words": wb_words, "wb_scales": wb_scales,
        "gain": gain.astype(np.float32),
        "wc": wc.astype(np.float32),
        "wgo": np.exp(0.3 * n((128, S))).astype(np.float32),
    }

def reference(tab_words, tab_scales, offs, offs2, offs3, wa, wb_words, wb_scales, gain, wc, wgo):
    TW = unpack_weight(tab_words, tab_scales, "e4m3")
    v = TW[:, unstriped(offs)]
    v2 = TW[:, unstriped(offs2)]
    wb = unpack_weight(wb_words, wb_scales, "e2m1")
    box = mxq(f64(wa), 0, "e4m3").T @ v
    truck = wb.T @ v2
    h = box / (1.0 + np.abs(box + truck))
    h = h * f64(gain)[:, None]
    y = np.tanh(mxq(f64(wc), 0, "e4m3").T @ mxq(h, 0, "e4m3"))
    out = np.zeros((N, T2))
    out[:, unstriped(offs3)] = np.tile(f64(wgo), (N // 128, 1)) * y
    return out

@@ -1,0 +1,259 @@
+from contextlib import ExitStack
+
+import concourse.mybir as mybir
+
+K, T, S, H, N, T2 = 512, 4096, 1024, 1024, 512, 2048
+FLOPS = 2 * K * H * S * 2 + 2 * H * N * S
+
+F32 = mybir.dt.float32
+BF16 = mybir.dt.bfloat16
+I32 = mybir.dt.int32
+U32 = mybir.dt.uint32
+U16 = mybir.dt.uint16
+U8 = mybir.dt.uint8
+FP8X4 = mybir.dt.float8_e4m3fn_x4
+FP4X4 = mybir.dt.float4_e2m1fn_x4
+ACT = mybir.ActivationFunctionType
+ALU = mybir.AluOpType
+
+P = 128
+PACK = 4
+PASS = P * PACK
+PASSES = H // PASS
+HALF = 512
+STRIP = 256
+CHUNKS = [(0, 256), (256, 256), (512, 512)]
+EVAC_V = {(2, 1), (2, 3)}
+V2_G = set()
+
+
+def tile_list_truck_box_appointment_kernel(
+    tc, tab_words, tab_scales, offs, offs2, offs3, wa, wb_words, wb_scales, gain, wc, wgo, out
+):
+    nc = tc.nc
+    with ExitStack() as ctx:
+        lists = ctx.enter_context(tc.tile_pool(name="lists", bufs=1))
+        keep = ctx.enter_context(tc.tile_pool(name="keep", bufs=1))
+        stage = ctx.enter_context(tc.tile_pool(name="stage", bufs=1))
+        work = ctx.enter_context(tc.tile_pool(name="work", bufs=3))
+        psum = ctx.enter_context(tc.psum_pool(name="psum", bufs=8))
+
+        tab_s = keep.tile([P, T], U8, name="tab_s", align_bytes=64)
+        nc.vector.memset(tab_s[:].bitcast(I32), 0)
+        wb_s_raw = keep.tile([P, H], U8, name="wb_s_raw", align_bytes=64)
+        nc.gpsimd.memset(wb_s_raw[:].bitcast(I32), 0)
+
+        box_list = lists.tile([P, S // 16], U16, name="box_list")
+        truck_list = lists.tile([P, S // 16], U16, name="truck_list")
+        slot_list = lists.tile([P, S // 16], U16, name="slot_list")
+        gains = keep.tile([P, PASSES, PACK], F32, name="gains")
+        nc.sync.dma_start(out=gains[:], in_=gain.rearrange("(b p t) -> p b t", b=PASSES, t=PACK))
+        nc.sync.dma_start(box_list[:], offs)
+        nc.sync.dma_start(truck_list[:], offs2)
+        nc.sync.dma_start(slot_list[:], offs3)
+        for q in range(4):
+            nc.scalar.dma_start(
+                out=tab_s[32 * q : 32 * q + 4, :].bitcast(I32), in_=tab_scales[0, 4 * q : 4 * q + 4, :].bitcast(I32)
+            )
+        for q in range(4):
+            nc.gpsimd.dma_start(
+                out=wb_s_raw[32 * q : 32 * q + 4, :].bitcast(I32), in_=wb_scales[0, 4 * q : 4 * q + 4, :].bitcast(I32)
+            )
+
+        wa_rows = wa.rearrange("(p j) c -> p j c", j=PACK)
+        wa_raw = []
+        wa_raw.append(stage.tile([P, PACK, PASS], F32, name="wa_raw0", tag="raw_a"))
+        nc.sync.dma_start(out=wa_raw[0][:], in_=wa_rows[:, :, 0:PASS])
+        wb_raw = stage.tile([P, 2 * H], U8, name="wb_raw", tag="raw_b")
+        nc.sync.dma_start(out=wb_raw[:].bitcast(I32), in_=wb_words[0].bitcast(I32))
+        tab_w = keep.tile([P, T], U32, name="tab_w", align_bytes=64)
+        nc.sync.dma_start(out=tab_w[:].bitcast(I32), in_=tab_words[0].rearrange("p t i -> p (t i)").bitcast(I32))
+
+        nonzero = keep.tile([P, PASSES, PACK], F32, name="nonzero")
+        nc.vector.scalar_tensor_tensor(nonzero[:], gains[:], 0.0, gains[:], ALU.is_equal, ALU.add)
+        root = keep.tile([P, PASSES, PACK], F32, name="root")
+        nc.scalar.activation(root[:], nonzero[:], ACT.Abs_reciprocal_sqrt)
+        nc.scalar.activation(root[:], root[:], ACT.Square)
+        signs = keep.tile([P, PASSES, PACK], F32, name="signs")
+        nc.scalar.activation(signs[:], nonzero[:], ACT.Sign)
+        guess = keep.tile([P, PASSES, PACK], F32, name="guess")
+        nc.vector.tensor_tensor(guess[:], root[:], signs[:], ALU.mult)
+        polish = keep.tile([P, PASSES, PACK], F32, name="polish")
+        nc.vector.tensor_tensor(polish[:], guess[:], nonzero[:], ALU.mult)
+        nc.vector.tensor_scalar(polish[:], polish[:], -1.0, 2.0, ALU.mult, ALU.add)
+        inv_gains = keep.tile([P, PASSES, PACK], F32, name="inv_gains")
+        nc.vector.tensor_tensor(inv_gains[:], guess[:], polish[:], ALU.mult)
+
+        pages = [keep.tile([P, T2], F32, name="page%d" % q) for q in range(N // P)]
+        for q in range(N // P):
+            if q < 2:
+                nc.vector.memset(pages[q][:], 0.0)
+            else:
+                nc.gpsimd.memset(pages[q][:], 0.0)
+
+        def quantise(grouped, width, name):
+            codes = keep.tile([P, width], U32, name=name + "_codes", align_bytes=64)
+            scales = keep.tile([P, width], U8, name=name + "_scales", align_bytes=64)
+            nc.vector.quantize_mx(out=codes[:].bitcast(FP8X4), scales=scales[:], in_=grouped[:])
+            return codes, scales
+
+        def group_wa(b, copy):
+            grouped = keep.tile([P, PASS * PACK], BF16, name="wa_grouped%d" % b, tag="wa_grouped%d" % b, align_bytes=64)
+            copy(
+                grouped[:].rearrange("p (t m j) -> p m j t", t=PACK, j=PACK),
+                wa_raw[b][:].rearrange("p j (m t) -> p m j t", t=PACK),
+            )
+            return grouped
+
+        def pool_cast(dst, src):
+            nc.gpsimd.tensor_scalar(dst, src, 1.0, 0.0, ALU.mult, ALU.add)
+
+        wa_q = [None, None]
+        wa_g0 = group_wa(0, nc.scalar.copy)
+        wa_raw.append(stage.tile([P, PACK, PASS], F32, name="wa_raw1", tag="raw_a"))
+        nc.sync.dma_start(out=wa_raw[1][:], in_=wa_rows[:, :, PASS : 2 * PASS])
+
+        wb_w = keep.tile([P, 2 * H], U8, name="wb_w", align_bytes=64)
+        nc.scalar.copy(
+            wb_w[:].bitcast(U16).rearrange("p (b t m) -> p b m t", b=PASSES, t=PACK),
+            wb_raw[:].bitcast(U16).rearrange("p (b m t) -> p b m t", b=PASSES, t=PACK),
+        )
+        wb_s = keep.tile([P, H], U8, name="wb_s", align_bytes=64)
+        nc.vector.tensor_copy(
+            wb_s[:].rearrange("p (b t m) -> p b t m", b=PASSES, t=PACK),
+            wb_s_raw[:].rearrange("p (b m t) -> p b t m", b=PASSES, t=PACK),
+        )
+
+        def gather_scales(offsets, half, name):
+            picked = keep.tile([P, HALF], U8, name="%s_scales%d" % (name, half), align_bytes=64)
+            cols = HALF // 16
+            nc.vector.tensor_copy(picked[:], tab_s[:].indirect(offsets[:, half * cols : (half + 1) * cols]))
+            return picked
+
+        box_scales = [gather_scales(box_list, 0, "box")]
+        truck_scales = [gather_scales(truck_list, 0, "truck")]
+        wa_q[0] = quantise(wa_g0, PASS, "wa0")
+        box_scales.append(gather_scales(box_list, 1, "box"))
+        truck_scales.append(gather_scales(truck_list, 1, "truck"))
+
+        words = {}
+
+        def gather_chunk(c, tag):
+            start, width = CHUNKS[c]
+            picked = keep.tile([P, 2, width], U32, name="words%d" % c, tag=tag, align_bytes=64)
+            cols = slice(start // 16, (start + width) // 16)
+            nc.vector.tensor_copy(picked[:, 0, :], tab_w[:].indirect(box_list[:, cols]))
+            nc.vector.tensor_copy(picked[:, 1, :], tab_w[:].indirect(truck_list[:, cols]))
+            words[c] = picked
+
+        wc_q = []
+
+        def prepare_wc(b):
+            raw = stage.tile([P, PACK, N], F32, name="wc_raw%d" % b, tag=("raw_b", "raw_a")[b])
+            nc.sync.dma_start(out=raw[:], in_=wc[b * PASS : (b + 1) * PASS, :].rearrange("(p t) n -> p t n", t=PACK))
+            grouped = keep.tile([P, N * PACK], BF16, name="wc_grouped%d" % b, align_bytes=64)
+            pool_cast(grouped[:].rearrange("p (n t) -> p n t", t=PACK), raw[:].rearrange("p t n -> p n t"))
+            wc_q.append(quantise(grouped, N, "wc%d" % b))
+
+        sums = {}
+
+        def first_stage(c, b):
+            start, width = CHUNKS[c]
+            half, at = divmod(start, HALF)
+            gained = keep.tile([P, PACK, width], F32, name="gained%d_%d" % (c, b))
+            damp = keep.tile([P, PACK, width], F32, name="damp%d_%d" % (c, b))
+            for t in range(PACK):
+                u = b * PACK + t
+                box = psum.tile([P, width], F32, name="box", tag="bank")
+                truck = psum.tile([P, width], F32, name="truck", tag="bank")
+                cols = slice(t * P, (t + 1) * P)
+                nc.tensor.matmul_mx(
+                    out=box[:], lhsT=wa_q[b][0][:, cols].bitcast(FP8X4), lhsT_scale=wa_q[b][1][:, cols],
+                    rhs=words[c][:, 0, :].bitcast(FP8X4), rhs_scale=box_scales[half][:, at : at + width],
+                    start=True, stop=True,
+                )
+                nc.tensor.matmul_mx(
+                    out=truck[:], lhsT=wb_w[:, 2 * u * P : 2 * (u + 1) * P].bitcast(FP4X4),
+                    lhsT_scale=wb_s[:, u * P : (u + 1) * P],
+                    rhs=words[c][:, 1, :].bitcast(FP8X4), rhs_scale=truck_scales[half][:, at : at + width],
+                    start=True, stop=True,
+                )
+                if (c, u) in EVAC_V:
+                    nc.vector.tensor_scalar(gained[:, t, :], box[:], gains[:, b, t : t + 1], None, ALU.mult)
+                else:
+                    nc.scalar.activation(gained[:, t, :], box[:], ACT.Copy, scale=gains[:, b, t : t + 1])
+                nc.vector.scalar_tensor_tensor(
+                    damp[:, t, :], gained[:, t, :], inv_gains[:, b, t : t + 1], truck[:], ALU.mult, ALU.add
+                )
+            for at in range(0, width, STRIP):
+                sums[(start + at) // STRIP, b] = (gained[:, :, at : at + STRIP], damp[:, :, at : at + STRIP])
+
+        h_q = {}
+        for half in range(S // HALF):
+            for b in range(PASSES):
+                h_q[half, b] = (
+                    keep.tile([P, HALF], U32, name="h_codes%d_%d" % (half, b), align_bytes=64),
+                    keep.tile([P, HALF], U8, name="h_scales%d_%d" % (half, b), align_bytes=64),
+                )
+
+        def damping(strip, b):
+            gained, damp = sums[strip, b]
+            nc.scalar.activation(damp, damp, ACT.Abs)
+            nc.scalar.activation(damp, damp, ACT.Abs_reciprocal_sqrt, bias=1.0)
+            nc.scalar.activation(damp, damp, ACT.Square)
+            h = work.tile([P, STRIP * PACK], BF16, name="h", tag="h", align_bytes=64)
+            engine = nc.gpsimd if (strip, b) in V2_G else nc.vector
+            engine.tensor_tensor(
+                h[:].rearrange("p (c i t) -> p c t i", i=4, t=PACK),
+                gained.rearrange("p t (c i) -> p c t i", i=4),
+                damp.rearrange("p t (c i) -> p c t i", i=4),
+                ALU.mult,
+            )
+            half, at = divmod(strip * STRIP, HALF)
+            codes, scales = h_q[half, b]
+            nc.vector.quantize_mx(
+                out=codes[:, at : at + STRIP].bitcast(FP8X4), scales=scales[:, at : at + STRIP], in_=h[:]
+            )
+
+        def second_stage(half):
+            cols = slice(half * HALF, (half + 1) * HALF)
+            offsets = slot_list[:, half * HALF // 16 : (half + 1) * HALF // 16]
+            accs = [psum.tile([P, HALF], F32, name="acc%d" % q, tag="bank") for q in range(N // P)]
+            for b in range(PASSES):
+                for q in range(N // P):
+                    rows = slice(q * P, (q + 1) * P)
+                    nc.tensor.matmul_mx(
+                        out=accs[q][:], lhsT=wc_q[b][0][:, rows].bitcast(FP8X4), lhsT_scale=wc_q[b][1][:, rows],
+                        rhs=h_q[half, b][0][:].bitcast(FP8X4), rhs_scale=h_q[half, b][1][:],
+                        start=(b == 0), stop=(b == PASSES - 1),
+                    )
+            for q in range(N // P):
+                y = work.tile([P, HALF], F32, name="y", tag="y", bufs=8)
+                nc.scalar.activation(y[:], accs[q][:], ACT.Tanh)
+                nc.vector.tensor_tensor(pages[q][:].indirect(offsets), y[:], factors[:, cols], ALU.mult)
+                if half == S // HALF - 1:
+                    nc.sync.dma_start(out=out[q * P : (q + 1) * P, :], in_=pages[q][:])
+
+        gather_chunk(0, "words0")
+        first_stage(0, 0)
+        gather_chunk(1, "words1")
+        first_stage(1, 0)
+        wa_q[1] = quantise(group_wa(1, nc.vector.tensor_copy), PASS, "wa1")
+        damping(0, 0)
+        first_stage(0, 1)
+        damping(1, 0)
+        prepare_wc(0)
+        prepare_wc(1)
+        factors = stage.tile([P, S], F32, name="factors", tag="raw_b")
+        nc.sync.dma_start(out=factors[:], in_=wgo)
+        first_stage(1, 1)
+        gather_chunk(2, "wa_grouped1")
+        damping(0, 1)
+        first_stage(2, 0)
+        damping(1, 1)
+        first_stage(2, 1)
+        second_stage(0)
+        for b in range(PASSES):
+            damping(2, b)
+            damping(3, b)
+        second_stage(1)

@@ -23,7 +23,7 @@ PASSES = H // PASS
 HALF = 512
 STRIP = 256
 CHUNKS = [(0, 256), (256, 256), (512, 512)]
-EVAC_V = {(2, 1), (2, 3)}
+EVAC_V = {(3, 0)}
 V2_G = set()
 
 
@@ -36,12 +36,12 @@ def tile_list_truck_box_appointment_kernel(
         keep = ctx.enter_context(tc.tile_pool(name="keep", bufs=1))
         stage = ctx.enter_context(tc.tile_pool(name="stage", bufs=1))
         work = ctx.enter_context(tc.tile_pool(name="work", bufs=3))
-        psum = ctx.enter_context(tc.psum_pool(name="psum", bufs=8))
+        psum = ctx.enter_context(tc.psum_pool(name="psum", bufs=4))
 
         tab_s = keep.tile([P, T], U8, name="tab_s", align_bytes=64)
         nc.vector.memset(tab_s[:].bitcast(I32), 0)
-        wb_s_raw = keep.tile([P, H], U8, name="wb_s_raw", align_bytes=64)
-        nc.gpsimd.memset(wb_s_raw[:].bitcast(I32), 0)
+        wb_s_raw = keep.tile([P, H], U8, name="wb_s_raw", tag="wb_s_raw", align_bytes=64)
+        nc.vector.memset(wb_s_raw[:].bitcast(I32), 0)
 
         box_list = lists.tile([P, S // 16], U16, name="box_list")
         truck_list = lists.tile([P, S // 16], U16, name="truck_list")
@@ -84,12 +84,9 @@ def tile_list_truck_box_appointment_kernel(
         inv_gains = keep.tile([P, PASSES, PACK], F32, name="inv_gains")
         nc.vector.tensor_tensor(inv_gains[:], guess[:], polish[:], ALU.mult)
 
-        pages = [keep.tile([P, T2], F32, name="page%d" % q) for q in range(N // P)]
-        for q in range(N // P):
-            if q < 2:
-                nc.vector.memset(pages[q][:], 0.0)
-            else:
-                nc.gpsimd.memset(pages[q][:], 0.0)
+        pages = [keep.tile([P, T2], F32, name="page%d" % q) for q in range(N // P - 1)]
+        for page in pages:
+            nc.vector.memset(page[:], 0.0)
 
         def quantise(grouped, width, name):
             codes = keep.tile([P, width], U32, name=name + "_codes", align_bytes=64)
@@ -118,23 +115,23 @@ def tile_list_truck_box_appointment_kernel(
             wb_w[:].bitcast(U16).rearrange("p (b t m) -> p b m t", b=PASSES, t=PACK),
             wb_raw[:].bitcast(U16).rearrange("p (b m t) -> p b m t", b=PASSES, t=PACK),
         )
-        wb_s = keep.tile([P, H], U8, name="wb_s", align_bytes=64)
-        nc.vector.tensor_copy(
-            wb_s[:].rearrange("p (b t m) -> p b t m", b=PASSES, t=PACK),
-            wb_s_raw[:].rearrange("p (b m t) -> p b t m", b=PASSES, t=PACK),
-        )
 
-        def gather_scales(offsets, half, name):
-            picked = keep.tile([P, HALF], U8, name="%s_scales%d" % (name, half), align_bytes=64)
+        def gather_scales(offsets, half, name, tag):
+            picked = keep.tile([P, HALF], U8, name="%s_scales%d" % (name, half), tag=tag, align_bytes=64)
             cols = HALF // 16
             nc.vector.tensor_copy(picked[:], tab_s[:].indirect(offsets[:, half * cols : (half + 1) * cols]))
             return picked
 
-        box_scales = [gather_scales(box_list, 0, "box")]
-        truck_scales = [gather_scales(truck_list, 0, "truck")]
+        box_scales = [gather_scales(box_list, 0, "box", "box_scales0")]
+        truck_scales = [gather_scales(truck_list, 0, "truck", "truck_scales0")]
         wa_q[0] = quantise(wa_g0, PASS, "wa0")
-        box_scales.append(gather_scales(box_list, 1, "box"))
-        truck_scales.append(gather_scales(truck_list, 1, "truck"))
+        box_scales.append(gather_scales(box_list, 1, "box", "box_scales1"))
+
+        wb_s = keep.tile([P, H], U8, name="wb_s", tag="wa_grouped0", align_bytes=64)
+        nc.vector.tensor_copy(
+            wb_s[:].rearrange("p (b t m) -> p b t m", b=PASSES, t=PACK),
+            wb_s_raw[:].rearrange("p (b m t) -> p b t m", b=PASSES, t=PACK),
+        )
 
         words = {}
 
@@ -151,42 +148,53 @@ def tile_list_truck_box_appointment_kernel(
         def prepare_wc(b):
             raw = stage.tile([P, PACK, N], F32, name="wc_raw%d" % b, tag=("raw_b", "raw_a")[b])
             nc.sync.dma_start(out=raw[:], in_=wc[b * PASS : (b + 1) * PASS, :].rearrange("(p t) n -> p t n", t=PACK))
-            grouped = keep.tile([P, N * PACK], BF16, name="wc_grouped%d" % b, align_bytes=64)
-            pool_cast(grouped[:].rearrange("p (n t) -> p n t", t=PACK), raw[:].rearrange("p t n -> p n t"))
+            grouped = keep.tile([P, N * PACK], BF16, name="wc_grouped%d" % b, tag="wc_grouped%d" % b, align_bytes=64)
+            nc.vector.tensor_copy(
+                grouped[:].rearrange("p (c i t) -> p c t i", i=4, t=PACK), raw[:].rearrange("p t (c i) -> p c t i", i=4)
+            )
             wc_q.append(quantise(grouped, N, "wc%d" % b))
 
         sums = {}
 
-        def first_stage(c, b):
-            start, width = CHUNKS[c]
-            half, at = divmod(start, HALF)
-            gained = keep.tile([P, PACK, width], F32, name="gained%d_%d" % (c, b))
-            damp = keep.tile([P, PACK, width], F32, name="damp%d_%d" % (c, b))
+        def first_stage(strip, b, summed):
+            half, at = divmod(strip * STRIP, HALF)
+            c = min(strip, 2)
+            within = strip * STRIP - CHUNKS[c][0]
+            box_words = words[c][:, 0, within : within + STRIP].bitcast(FP8X4)
+            truck_words = words[c][:, 1, within : within + STRIP].bitcast(FP8X4)
+            gained = keep.tile([P, PACK, STRIP], F32, name="gained%d_%d" % (strip, b))
+            damp = keep.tile([P, PACK, STRIP], F32, name="damp%d_%d" % (strip, b), tag="damp%d_%d" % (strip, b))
             for t in range(PACK):
                 u = b * PACK + t
-                box = psum.tile([P, width], F32, name="box", tag="bank")
-                truck = psum.tile([P, width], F32, name="truck", tag="bank")
+                bank = psum.tile([P, 2, STRIP], F32, name="bank", tag="unit")
                 cols = slice(t * P, (t + 1) * P)
+
+                def box_pass(place, stop):
+                    nc.tensor.matmul_mx(
+                        out=place, lhsT=wa_q[b][0][:, cols].bitcast(FP8X4), lhsT_scale=wa_q[b][1][:, cols],
+                        rhs=box_words, rhs_scale=box_scales[half][:, at : at + STRIP], start=True, stop=stop,
+                    )
+
+                box_pass(bank[:, 1, :], True)
+                if summed:
+                    box_pass(bank[:, 0, :], False)
                 nc.tensor.matmul_mx(
-                    out=box[:], lhsT=wa_q[b][0][:, cols].bitcast(FP8X4), lhsT_scale=wa_q[b][1][:, cols],
-                    rhs=words[c][:, 0, :].bitcast(FP8X4), rhs_scale=box_scales[half][:, at : at + width],
-                    start=True, stop=True,
-                )
-                nc.tensor.matmul_mx(
-                    out=truck[:], lhsT=wb_w[:, 2 * u * P : 2 * (u + 1) * P].bitcast(FP4X4),
+                    out=bank[:, 0, :], lhsT=wb_w[:, 2 * u * P : 2 * (u + 1) * P].bitcast(FP4X4),
                     lhsT_scale=wb_s[:, u * P : (u + 1) * P],
-                    rhs=words[c][:, 1, :].bitcast(FP8X4), rhs_scale=truck_scales[half][:, at : at + width],
-                    start=True, stop=True,
+                    rhs=truck_words, rhs_scale=truck_scales[half][:, at : at + STRIP],
+                    start=not summed, stop=True,
                 )
-                if (c, u) in EVAC_V:
-                    nc.vector.tensor_scalar(gained[:, t, :], box[:], gains[:, b, t : t + 1], None, ALU.mult)
+                if (strip, b) in EVAC_V:
+                    nc.vector.tensor_scalar(gained[:, t, :], bank[:, 1, :], gains[:, b, t : t + 1], None, ALU.mult)
                 else:
-                    nc.scalar.activation(gained[:, t, :], box[:], ACT.Copy, scale=gains[:, b, t : t + 1])
-                nc.vector.scalar_tensor_tensor(
-                    damp[:, t, :], gained[:, t, :], inv_gains[:, b, t : t + 1], truck[:], ALU.mult, ALU.add
-                )
-            for at in range(0, width, STRIP):
-                sums[(start + at) // STRIP, b] = (gained[:, :, at : at + STRIP], damp[:, :, at : at + STRIP])
+                    nc.scalar.activation(gained[:, t, :], bank[:, 1, :], ACT.Copy, scale=gains[:, b, t : t + 1])
+                if summed:
+                    nc.scalar.activation(damp[:, t, :], bank[:, 0, :], ACT.Abs)
+                else:
+                    nc.vector.scalar_tensor_tensor(
+                        damp[:, t, :], gained[:, t, :], inv_gains[:, b, t : t + 1], bank[:, 0, :], ALU.mult, ALU.add
+                    )
+            sums[strip, b] = (gained[:], damp[:], summed)
 
         h_q = {}
         for half in range(S // HALF):
@@ -197,8 +205,9 @@ def tile_list_truck_box_appointment_kernel(
                 )
 
         def damping(strip, b):
-            gained, damp = sums[strip, b]
-            nc.scalar.activation(damp, damp, ACT.Abs)
+            gained, damp, summed = sums[strip, b]
+            if not summed:
+                nc.scalar.activation(damp, damp, ACT.Abs)
             nc.scalar.activation(damp, damp, ACT.Abs_reciprocal_sqrt, bias=1.0)
             nc.scalar.activation(damp, damp, ACT.Square)
             h = work.tile([P, STRIP * PACK], BF16, name="h", tag="h", align_bytes=64)
@@ -218,7 +227,7 @@ def tile_list_truck_box_appointment_kernel(
         def second_stage(half):
             cols = slice(half * HALF, (half + 1) * HALF)
             offsets = slot_list[:, half * HALF // 16 : (half + 1) * HALF // 16]
-            accs = [psum.tile([P, HALF], F32, name="acc%d" % q, tag="bank") for q in range(N // P)]
+            accs = [psum.tile([P, HALF], F32, name="acc%d" % q, tag="acc") for q in range(N // P)]
             for b in range(PASSES):
                 for q in range(N // P):
                     rows = slice(q * P, (q + 1) * P)
@@ -235,25 +244,31 @@ def tile_list_truck_box_appointment_kernel(
                     nc.sync.dma_start(out=out[q * P : (q + 1) * P, :], in_=pages[q][:])
 
         gather_chunk(0, "words0")
-        first_stage(0, 0)
-        gather_chunk(1, "words1")
-        first_stage(1, 0)
+        first_stage(0, 0, True)
+        gather_chunk(1, "wb_s_raw")
+        first_stage(1, 0, False)
         wa_q[1] = quantise(group_wa(1, nc.vector.tensor_copy), PASS, "wa1")
         damping(0, 0)
-        first_stage(0, 1)
+        first_stage(0, 1, False)
         damping(1, 0)
         prepare_wc(0)
         prepare_wc(1)
         factors = stage.tile([P, S], F32, name="factors", tag="raw_b")
         nc.sync.dma_start(out=factors[:], in_=wgo)
-        first_stage(1, 1)
+        first_stage(1, 1, False)
+        truck_scales.append(gather_scales(truck_list, 1, "truck", "wc_grouped0"))
         gather_chunk(2, "wa_grouped1")
         damping(0, 1)
-        first_stage(2, 0)
+        first_stage(2, 0, False)
         damping(1, 1)
-        first_stage(2, 1)
+        pages.append(keep.tile([P, T2], F32, name="page3", tag="damp1_1"))
+        nc.gpsimd.memset(pages[3][:], 0.0)
+        first_stage(3, 0, False)
+        first_stage(2, 1, False)
         second_stage(0)
-        for b in range(PASSES):
-            damping(2, b)
-            damping(3, b)
+        damping(2, 0)
+        damping(3, 0)
+        first_stage(3, 1, True)
+        damping(2, 1)
+        damping(3, 1)
         second_stage(1)

@@ -23,7 +23,7 @@ PASSES = H // PASS
 HALF = 512
 STRIP = 256
 CHUNKS = [(0, 256), (256, 256), (512, 512)]
-EVAC_V = {(3, 0)}
+EVAC_V = {(512, 0, 0), (512, 0, 1), (512, 0, 2), (512, 0, 3)}
 V2_G = set()
 
 
@@ -84,9 +84,9 @@ def tile_list_truck_box_appointment_kernel(
         inv_gains = keep.tile([P, PASSES, PACK], F32, name="inv_gains")
         nc.vector.tensor_tensor(inv_gains[:], guess[:], polish[:], ALU.mult)
 
-        pages = [keep.tile([P, T2], F32, name="page%d" % q) for q in range(N // P - 1)]
+        pages = [keep.tile([P, T2], F32, name="page%d" % q) for q in range(N // P)]
         for page in pages:
-            nc.vector.memset(page[:], 0.0)
+            nc.vector.memset(page[:].bitcast(I32), 0)
 
         def quantise(grouped, width, name):
             codes = keep.tile([P, width], U32, name=name + "_codes", align_bytes=64)
@@ -104,6 +104,10 @@ def tile_list_truck_box_appointment_kernel(
 
         def pool_cast(dst, src):
             nc.gpsimd.tensor_scalar(dst, src, 1.0, 0.0, ALU.mult, ALU.add)
+
+        def pool_group_wa(dst, src):
+            for t in range(PACK):
+                pool_cast(dst[:, :, :, t], src[:, :, :, t])
 
         wa_q = [None, None]
         wa_g0 = group_wa(0, nc.scalar.copy)
@@ -135,13 +139,11 @@ def tile_list_truck_box_appointment_kernel(
 
         words = {}
 
-        def gather_chunk(c, tag):
-            start, width = CHUNKS[c]
-            picked = keep.tile([P, 2, width], U32, name="words%d" % c, tag=tag, align_bytes=64)
+        def gather_words(start, width):
+            half, at = divmod(start, HALF)
             cols = slice(start // 16, (start + width) // 16)
-            nc.vector.tensor_copy(picked[:, 0, :], tab_w[:].indirect(box_list[:, cols]))
-            nc.vector.tensor_copy(picked[:, 1, :], tab_w[:].indirect(truck_list[:, cols]))
-            words[c] = picked
+            nc.vector.tensor_copy(words[half][:, 0, at : at + width], tab_w[:].indirect(box_list[:, cols]))
+            nc.vector.tensor_copy(words[half][:, 1, at : at + width], tab_w[:].indirect(truck_list[:, cols]))
 
         wc_q = []
 
@@ -149,52 +151,57 @@ def tile_list_truck_box_appointment_kernel(
             raw = stage.tile([P, PACK, N], F32, name="wc_raw%d" % b, tag=("raw_b", "raw_a")[b])
             nc.sync.dma_start(out=raw[:], in_=wc[b * PASS : (b + 1) * PASS, :].rearrange("(p t) n -> p t n", t=PACK))
             grouped = keep.tile([P, N * PACK], BF16, name="wc_grouped%d" % b, tag="wc_grouped%d" % b, align_bytes=64)
-            nc.vector.tensor_copy(
-                grouped[:].rearrange("p (c i t) -> p c t i", i=4, t=PACK), raw[:].rearrange("p t (c i) -> p c t i", i=4)
-            )
+            for n0 in range(0, N, P):
+                pool_cast(
+                    grouped[:, n0 * PACK : (n0 + P) * PACK].rearrange("p (n t) -> p n t", t=PACK),
+                    raw[:, :, n0 : n0 + P].rearrange("p t n -> p n t"),
+                )
             wc_q.append(quantise(grouped, N, "wc%d" % b))
 
         sums = {}
 
-        def first_stage(strip, b, summed):
-            half, at = divmod(strip * STRIP, HALF)
-            c = min(strip, 2)
-            within = strip * STRIP - CHUNKS[c][0]
-            box_words = words[c][:, 0, within : within + STRIP].bitcast(FP8X4)
-            truck_words = words[c][:, 1, within : within + STRIP].bitcast(FP8X4)
-            gained = keep.tile([P, PACK, STRIP], F32, name="gained%d_%d" % (strip, b))
-            damp = keep.tile([P, PACK, STRIP], F32, name="damp%d_%d" % (strip, b), tag="damp%d_%d" % (strip, b))
+        def first_stage(start, width, b, summed):
+            half, at = divmod(start, HALF)
+            box_words = words[half][:, 0, at : at + width].bitcast(FP8X4)
+            truck_words = words[half][:, 1, at : at + width].bitcast(FP8X4)
+            gained = keep.tile([P, PACK, width], F32, name="gained%d_%d" % (start, b))
+            damp = keep.tile([P, PACK, width], F32, name="damp%d_%d" % (start, b), tag="damp%d_%d" % (start, b))
             for t in range(PACK):
                 u = b * PACK + t
-                bank = psum.tile([P, 2, STRIP], F32, name="bank", tag="unit")
+                if width == HALF:
+                    other = psum.tile([P, width], F32, name="other", tag="unit")[:]
+                    box = psum.tile([P, width], F32, name="box", tag="unit")[:]
+                else:
+                    bank = psum.tile([P, 2, width], F32, name="bank", tag="unit")
+                    other, box = bank[:, 0, :], bank[:, 1, :]
                 cols = slice(t * P, (t + 1) * P)
 
                 def box_pass(place, stop):
                     nc.tensor.matmul_mx(
                         out=place, lhsT=wa_q[b][0][:, cols].bitcast(FP8X4), lhsT_scale=wa_q[b][1][:, cols],
-                        rhs=box_words, rhs_scale=box_scales[half][:, at : at + STRIP], start=True, stop=stop,
+                        rhs=box_words, rhs_scale=box_scales[half][:, at : at + width], start=True, stop=stop,
                     )
 
-                box_pass(bank[:, 1, :], True)
+                box_pass(box, True)
                 if summed:
-                    box_pass(bank[:, 0, :], False)
+                    box_pass(other, False)
                 nc.tensor.matmul_mx(
-                    out=bank[:, 0, :], lhsT=wb_w[:, 2 * u * P : 2 * (u + 1) * P].bitcast(FP4X4),
+                    out=other, lhsT=wb_w[:, 2 * u * P : 2 * (u + 1) * P].bitcast(FP4X4),
                     lhsT_scale=wb_s[:, u * P : (u + 1) * P],
-                    rhs=truck_words, rhs_scale=truck_scales[half][:, at : at + STRIP],
+                    rhs=truck_words, rhs_scale=truck_scales[half][:, at : at + width],
                     start=not summed, stop=True,
                 )
-                if (strip, b) in EVAC_V:
-                    nc.vector.tensor_scalar(gained[:, t, :], bank[:, 1, :], gains[:, b, t : t + 1], None, ALU.mult)
+                if (start, b, t) in EVAC_V:
+                    nc.vector.tensor_scalar(gained[:, t, :], box, gains[:, b, t : t + 1], None, ALU.mult)
                 else:
-                    nc.scalar.activation(gained[:, t, :], bank[:, 1, :], ACT.Copy, scale=gains[:, b, t : t + 1])
+                    nc.scalar.activation(gained[:, t, :], box, ACT.Copy, scale=gains[:, b, t : t + 1])
                 if summed:
-                    nc.scalar.activation(damp[:, t, :], bank[:, 0, :], ACT.Abs)
+                    nc.scalar.activation(damp[:, t, :], other, ACT.Abs)
                 else:
                     nc.vector.scalar_tensor_tensor(
-                        damp[:, t, :], gained[:, t, :], inv_gains[:, b, t : t + 1], bank[:, 0, :], ALU.mult, ALU.add
+                        damp[:, t, :], gained[:, t, :], inv_gains[:, b, t : t + 1], other, ALU.mult, ALU.add
                     )
-            sums[strip, b] = (gained[:], damp[:], summed)
+            return start, b, gained, damp, summed
 
         h_q = {}
         for half in range(S // HALF):
@@ -204,29 +211,32 @@ def tile_list_truck_box_appointment_kernel(
                     keep.tile([P, HALF], U8, name="h_scales%d_%d" % (half, b), align_bytes=64),
                 )
 
-        def damping(strip, b):
-            gained, damp, summed = sums[strip, b]
+        def damping(sums, skip, width):
+            start, b, gained, damp, summed = sums
+            gained, damp = gained[:, :, skip : skip + width], damp[:, :, skip : skip + width]
             if not summed:
                 nc.scalar.activation(damp, damp, ACT.Abs)
             nc.scalar.activation(damp, damp, ACT.Abs_reciprocal_sqrt, bias=1.0)
             nc.scalar.activation(damp, damp, ACT.Square)
-            h = work.tile([P, STRIP * PACK], BF16, name="h", tag="h", align_bytes=64)
-            engine = nc.gpsimd if (strip, b) in V2_G else nc.vector
-            engine.tensor_tensor(
+            h = work.tile([P, width * PACK], BF16, name="h", tag="h", align_bytes=64)
+            nc.vector.tensor_tensor(
                 h[:].rearrange("p (c i t) -> p c t i", i=4, t=PACK),
                 gained.rearrange("p t (c i) -> p c t i", i=4),
                 damp.rearrange("p t (c i) -> p c t i", i=4),
                 ALU.mult,
             )
-            half, at = divmod(strip * STRIP, HALF)
+            half, at = divmod(start + skip, HALF)
             codes, scales = h_q[half, b]
             nc.vector.quantize_mx(
-                out=codes[:, at : at + STRIP].bitcast(FP8X4), scales=scales[:, at : at + STRIP], in_=h[:]
+                out=codes[:, at : at + width].bitcast(FP8X4), scales=scales[:, at : at + width], in_=h[:]
             )
 
-        def second_stage(half):
-            cols = slice(half * HALF, (half + 1) * HALF)
+        def place(half, q, y):
             offsets = slot_list[:, half * HALF // 16 : (half + 1) * HALF // 16]
+            cols = slice(half * HALF, (half + 1) * HALF)
+            nc.vector.tensor_tensor(pages[q][:].indirect(offsets), y[:], factors[:, cols], ALU.mult)
+
+        def second_stage(half):
             accs = [psum.tile([P, HALF], F32, name="acc%d" % q, tag="acc") for q in range(N // P)]
             for b in range(PASSES):
                 for q in range(N // P):
@@ -236,39 +246,40 @@ def tile_list_truck_box_appointment_kernel(
                         rhs=h_q[half, b][0][:].bitcast(FP8X4), rhs_scale=h_q[half, b][1][:],
                         start=(b == 0), stop=(b == PASSES - 1),
                     )
+            ys = []
             for q in range(N // P):
-                y = work.tile([P, HALF], F32, name="y", tag="y", bufs=8)
-                nc.scalar.activation(y[:], accs[q][:], ACT.Tanh)
-                nc.vector.tensor_tensor(pages[q][:].indirect(offsets), y[:], factors[:, cols], ALU.mult)
-                if half == S // HALF - 1:
-                    nc.sync.dma_start(out=out[q * P : (q + 1) * P, :], in_=pages[q][:])
+                ys.append(work.tile([P, HALF], F32, name="y", tag="y", bufs=8))
+                nc.scalar.activation(ys[q][:], accs[q][:], ACT.Tanh)
+            return ys
 
-        gather_chunk(0, "words0")
-        first_stage(0, 0, True)
-        gather_chunk(1, "wb_s_raw")
-        first_stage(1, 0, False)
-        wa_q[1] = quantise(group_wa(1, nc.vector.tensor_copy), PASS, "wa1")
-        damping(0, 0)
-        first_stage(0, 1, False)
-        damping(1, 0)
+        words[0] = keep.tile([P, 2, HALF], U32, name="words0", align_bytes=64)
+        gather_words(0, 256)
+        a0 = first_stage(0, 256, 0, True)
+        gather_words(256, 256)
+        a1 = first_stage(256, 256, 0, False)
+        wa_q[1] = quantise(group_wa(1, pool_group_wa), PASS, "wa1")
+        damping(a0, 0, 256)
+        a2 = first_stage(0, 512, 1, False)
+        damping(a1, 0, 256)
         prepare_wc(0)
         prepare_wc(1)
         factors = stage.tile([P, S], F32, name="factors", tag="raw_b")
         nc.sync.dma_start(out=factors[:], in_=wgo)
-        first_stage(1, 1, False)
         truck_scales.append(gather_scales(truck_list, 1, "truck", "wc_grouped0"))
-        gather_chunk(2, "wa_grouped1")
-        damping(0, 1)
-        first_stage(2, 0, False)
-        damping(1, 1)
-        pages.append(keep.tile([P, T2], F32, name="page3", tag="damp1_1"))
-        nc.gpsimd.memset(pages[3][:], 0.0)
-        first_stage(3, 0, False)
-        first_stage(2, 1, False)
-        second_stage(0)
-        damping(2, 0)
-        damping(3, 0)
-        first_stage(3, 1, True)
-        damping(2, 1)
-        damping(3, 1)
-        second_stage(1)
+        words[1] = keep.tile([P, 2, HALF], U32, name="words1", tag="wa_grouped1", align_bytes=64)
+        gather_words(512, 512)
+        damping(a2, 0, 256)
+        b0 = first_stage(512, 512, 0, False)
+        damping(a2, 256, 256)
+        b1 = first_stage(512, 256, 1, False)
+        ys = second_stage(0)
+        for q in range(4):
+            place(0, q, ys[q])
+        damping(b0, 0, 512)
+        b2 = first_stage(768, 256, 1, True)
+        damping(b1, 0, 256)
+        damping(b2, 0, 256)
+        ys = second_stage(1)
+        for q in range(4):
+            place(1, q, ys[q])
+            nc.sync.dma_start(out=out[q * P : (q + 1) * P, :], in_=pages[q][:])

@@ -23,7 +23,7 @@ PASSES = H // PASS
 HALF = 512
 STRIP = 256
 CHUNKS = [(0, 256), (256, 256), (512, 512)]
-EVAC_V = {(512, 0, 0), (512, 0, 1), (512, 0, 2), (512, 0, 3)}
+EVAC_V = {(512, 0, 1), (512, 0, 3)}
 V2_G = set()
 
 
@@ -84,7 +84,7 @@ def tile_list_truck_box_appointment_kernel(
         inv_gains = keep.tile([P, PASSES, PACK], F32, name="inv_gains")
         nc.vector.tensor_tensor(inv_gains[:], guess[:], polish[:], ALU.mult)
 
-        pages = [keep.tile([P, T2], F32, name="page%d" % q) for q in range(N // P)]
+        pages = [keep.tile([P, T2], F32, name="page%d" % q) for q in range(1)]
         for page in pages:
             nc.vector.memset(page[:].bitcast(I32), 0)
 
@@ -207,18 +207,18 @@ def tile_list_truck_box_appointment_kernel(
         for half in range(S // HALF):
             for b in range(PASSES):
                 h_q[half, b] = (
-                    keep.tile([P, HALF], U32, name="h_codes%d_%d" % (half, b), align_bytes=64),
-                    keep.tile([P, HALF], U8, name="h_scales%d_%d" % (half, b), align_bytes=64),
+                    keep.tile([P, HALF], U32, name="h_codes%d_%d" % (half, b), tag="h_codes%d_%d" % (half, b), align_bytes=64),
+                    keep.tile([P, HALF], U8, name="h_scales%d_%d" % (half, b), tag="h_scales%d_%d" % (half, b), align_bytes=64),
                 )
 
-        def damping(sums, skip, width):
+        def damping(sums, skip, width, pool=work, tag="h"):
             start, b, gained, damp, summed = sums
             gained, damp = gained[:, :, skip : skip + width], damp[:, :, skip : skip + width]
             if not summed:
                 nc.scalar.activation(damp, damp, ACT.Abs)
             nc.scalar.activation(damp, damp, ACT.Abs_reciprocal_sqrt, bias=1.0)
             nc.scalar.activation(damp, damp, ACT.Square)
-            h = work.tile([P, width * PACK], BF16, name="h", tag="h", align_bytes=64)
+            h = pool.tile([P, width * PACK], BF16, name="h", tag=tag, align_bytes=64)
             nc.vector.tensor_tensor(
                 h[:].rearrange("p (c i t) -> p c t i", i=4, t=PACK),
                 gained.rearrange("p t (c i) -> p c t i", i=4),
@@ -270,9 +270,12 @@ def tile_list_truck_box_appointment_kernel(
         gather_words(512, 512)
         damping(a2, 0, 256)
         b0 = first_stage(512, 512, 0, False)
-        damping(a2, 256, 256)
+        damping(a2, 256, 256, keep, "h_last")
         b1 = first_stage(512, 256, 1, False)
         ys = second_stage(0)
+        for q, tag in enumerate(("h_last", "h_codes0_1", "h_scales0_1")):
+            pages.append(keep.tile([P, T2], F32, name="page%d" % (q + 1), tag=tag, align_bytes=64))
+            nc.gpsimd.memset(pages[q + 1][:], 0.0)
         for q in range(4):
             place(0, q, ys[q])
         damping(b0, 0, 512)

@@ -20,11 +20,14 @@ P = 128
 PACK = 4
 PASS = P * PACK
 PASSES = H // PASS
-HALF = 512
-STRIP = 256
-CHUNKS = [(0, 256), (256, 256), (512, 512)]
-EVAC_V = {(512, 0, 1), (512, 0, 3)}
-V2_G = set()
+QUADRANTS = 4
+PER_COLUMN = 16
+HALF = S // 2
+STRIP = HALF // 2
+PAGES = N // P
+LINE = 4
+ACC_BANKS = PAGES
+BOX_READS_ON_VECTOR = 3
 
 
 def tile_list_truck_box_appointment_kernel(
@@ -36,34 +39,38 @@ def tile_list_truck_box_appointment_kernel(
         keep = ctx.enter_context(tc.tile_pool(name="keep", bufs=1))
         stage = ctx.enter_context(tc.tile_pool(name="stage", bufs=1))
         work = ctx.enter_context(tc.tile_pool(name="work", bufs=3))
-        psum = ctx.enter_context(tc.psum_pool(name="psum", bufs=4))
+        psum = ctx.enter_context(tc.psum_pool(name="psum", bufs=ACC_BANKS))
 
         tab_s = keep.tile([P, T], U8, name="tab_s", align_bytes=64)
         nc.vector.memset(tab_s[:].bitcast(I32), 0)
-        wb_s_raw = keep.tile([P, H], U8, name="wb_s_raw", tag="wb_s_raw", align_bytes=64)
+        wb_s_raw = keep.tile([P, H], U8, name="wb_s_raw", align_bytes=64)
         nc.vector.memset(wb_s_raw[:].bitcast(I32), 0)
 
-        box_list = lists.tile([P, S // 16], U16, name="box_list")
-        truck_list = lists.tile([P, S // 16], U16, name="truck_list")
-        slot_list = lists.tile([P, S // 16], U16, name="slot_list")
+        box_list = lists.tile([P, S // PER_COLUMN], U16, name="box_list")
+        truck_list = lists.tile([P, S // PER_COLUMN], U16, name="truck_list")
+        slot_list = lists.tile([P, S // PER_COLUMN], U16, name="slot_list")
         gains = keep.tile([P, PASSES, PACK], F32, name="gains")
-        nc.sync.dma_start(out=gains[:], in_=gain.rearrange("(b p t) -> p b t", b=PASSES, t=PACK))
+        nc.scalar.dma_start(out=gains[:], in_=gain.rearrange("(b p t) -> p b t", b=PASSES, t=PACK))
         nc.sync.dma_start(box_list[:], offs)
         nc.sync.dma_start(truck_list[:], offs2)
         nc.sync.dma_start(slot_list[:], offs3)
-        for q in range(4):
-            nc.scalar.dma_start(
+        for q in range(QUADRANTS):
+            nc.sync.dma_start(
                 out=tab_s[32 * q : 32 * q + 4, :].bitcast(I32), in_=tab_scales[0, 4 * q : 4 * q + 4, :].bitcast(I32)
             )
-        for q in range(4):
+        for q in range(QUADRANTS):
             nc.gpsimd.dma_start(
                 out=wb_s_raw[32 * q : 32 * q + 4, :].bitcast(I32), in_=wb_scales[0, 4 * q : 4 * q + 4, :].bitcast(I32)
             )
 
         wa_rows = wa.rearrange("(p j) c -> p j c", j=PACK)
-        wa_raw = []
-        wa_raw.append(stage.tile([P, PACK, PASS], F32, name="wa_raw0", tag="raw_a"))
-        nc.sync.dma_start(out=wa_raw[0][:], in_=wa_rows[:, :, 0:PASS])
+
+        def load_wa(b):
+            raw = stage.tile([P, PACK, PASS], F32, name="wa_raw%d" % b, tag="raw_a")
+            nc.sync.dma_start(out=raw[:], in_=wa_rows[:, :, b * PASS : (b + 1) * PASS])
+            return raw
+
+        wa_raw = [load_wa(0)]
         wb_raw = stage.tile([P, 2 * H], U8, name="wb_raw", tag="raw_b")
         nc.sync.dma_start(out=wb_raw[:].bitcast(I32), in_=wb_words[0].bitcast(I32))
         tab_w = keep.tile([P, T], U32, name="tab_w", align_bytes=64)
@@ -71,22 +78,26 @@ def tile_list_truck_box_appointment_kernel(
 
         nonzero = keep.tile([P, PASSES, PACK], F32, name="nonzero")
         nc.vector.scalar_tensor_tensor(nonzero[:], gains[:], 0.0, gains[:], ALU.is_equal, ALU.add)
-        root = keep.tile([P, PASSES, PACK], F32, name="root")
-        nc.scalar.activation(root[:], nonzero[:], ACT.Abs_reciprocal_sqrt)
-        nc.scalar.activation(root[:], root[:], ACT.Square)
+        inv_size = keep.tile([P, PASSES, PACK], F32, name="inv_size")
+        nc.scalar.activation(inv_size[:], nonzero[:], ACT.Abs_reciprocal_sqrt)
+        nc.scalar.activation(inv_size[:], inv_size[:], ACT.Square)
         signs = keep.tile([P, PASSES, PACK], F32, name="signs")
         nc.scalar.activation(signs[:], nonzero[:], ACT.Sign)
         guess = keep.tile([P, PASSES, PACK], F32, name="guess")
-        nc.vector.tensor_tensor(guess[:], root[:], signs[:], ALU.mult)
+        nc.vector.tensor_tensor(guess[:], inv_size[:], signs[:], ALU.mult)
         polish = keep.tile([P, PASSES, PACK], F32, name="polish")
         nc.vector.tensor_tensor(polish[:], guess[:], nonzero[:], ALU.mult)
         nc.vector.tensor_scalar(polish[:], polish[:], -1.0, 2.0, ALU.mult, ALU.add)
         inv_gains = keep.tile([P, PASSES, PACK], F32, name="inv_gains")
         nc.vector.tensor_tensor(inv_gains[:], guess[:], polish[:], ALU.mult)
 
-        pages = [keep.tile([P, T2], F32, name="page%d" % q) for q in range(1)]
-        for page in pages:
-            nc.vector.memset(page[:].bitcast(I32), 0)
+        pages = [keep.tile([P, T2], F32, name="page0")]
+        nc.vector.memset(pages[0][:].bitcast(I32), 0)
+
+        def clear_page(tag):
+            page = keep.tile([P, T2], F32, name="page%d" % len(pages), tag=tag, align_bytes=64)
+            nc.gpsimd.memset(page[:], 0.0)
+            pages.append(page)
 
         def quantise(grouped, width, name):
             codes = keep.tile([P, width], U32, name=name + "_codes", align_bytes=64)
@@ -94,42 +105,41 @@ def tile_list_truck_box_appointment_kernel(
             nc.vector.quantize_mx(out=codes[:].bitcast(FP8X4), scales=scales[:], in_=grouped[:])
             return codes, scales
 
-        def group_wa(b, copy):
+        def group_wa(b, cast):
             grouped = keep.tile([P, PASS * PACK], BF16, name="wa_grouped%d" % b, tag="wa_grouped%d" % b, align_bytes=64)
-            copy(
-                grouped[:].rearrange("p (t m j) -> p m j t", t=PACK, j=PACK),
-                wa_raw[b][:].rearrange("p j (m t) -> p m j t", t=PACK),
+            cast(
+                grouped[:].rearrange("p (t m j) -> p m t j", t=PACK, j=PACK),
+                wa_raw[b][:].rearrange("p j (m t) -> p m t j", t=PACK),
             )
             return grouped
 
-        def pool_cast(dst, src):
+        def gpsimd_cast(dst, src):
             nc.gpsimd.tensor_scalar(dst, src, 1.0, 0.0, ALU.mult, ALU.add)
 
-        def pool_group_wa(dst, src):
+        def gpsimd_cast_by_t(dst, src):
             for t in range(PACK):
-                pool_cast(dst[:, :, :, t], src[:, :, :, t])
+                gpsimd_cast(dst[:, :, t, :], src[:, :, t, :])
 
-        wa_q = [None, None]
-        wa_g0 = group_wa(0, nc.scalar.copy)
-        wa_raw.append(stage.tile([P, PACK, PASS], F32, name="wa_raw1", tag="raw_a"))
-        nc.sync.dma_start(out=wa_raw[1][:], in_=wa_rows[:, :, PASS : 2 * PASS])
+        wa_grouped = group_wa(0, nc.scalar.copy)
+        wa_raw.append(load_wa(1))
 
         wb_w = keep.tile([P, 2 * H], U8, name="wb_w", align_bytes=64)
         nc.scalar.copy(
-            wb_w[:].bitcast(U16).rearrange("p (b t m) -> p b m t", b=PASSES, t=PACK),
-            wb_raw[:].bitcast(U16).rearrange("p (b m t) -> p b m t", b=PASSES, t=PACK),
+            wb_w[:].bitcast(U16).rearrange("p (b t m) -> p b t m", b=PASSES, t=PACK),
+            wb_raw[:].bitcast(U16).rearrange("p (b m t) -> p b t m", b=PASSES, t=PACK),
         )
 
-        def gather_scales(offsets, half, name, tag):
-            picked = keep.tile([P, HALF], U8, name="%s_scales%d" % (name, half), tag=tag, align_bytes=64)
-            cols = HALF // 16
+        def gather_scales(offsets, half, name):
+            picked = keep.tile([P, HALF], U8, name="%s_scales%d" % (name, half), align_bytes=64)
+            cols = HALF // PER_COLUMN
             nc.vector.tensor_copy(picked[:], tab_s[:].indirect(offsets[:, half * cols : (half + 1) * cols]))
             return picked
 
-        box_scales = [gather_scales(box_list, 0, "box", "box_scales0")]
-        truck_scales = [gather_scales(truck_list, 0, "truck", "truck_scales0")]
-        wa_q[0] = quantise(wa_g0, PASS, "wa0")
-        box_scales.append(gather_scales(box_list, 1, "box", "box_scales1"))
+        box_scales = [gather_scales(box_list, 0, "box")]
+        truck_scales = [gather_scales(truck_list, 0, "truck")]
+        wa_q = [quantise(wa_grouped, PASS, "wa0")]
+        box_scales.append(gather_scales(box_list, 1, "box"))
+        truck_scales.append(gather_scales(truck_list, 1, "truck"))
 
         wb_s = keep.tile([P, H], U8, name="wb_s", tag="wa_grouped0", align_bytes=64)
         nc.vector.tensor_copy(
@@ -137,11 +147,11 @@ def tile_list_truck_box_appointment_kernel(
             wb_s_raw[:].rearrange("p (b m t) -> p b t m", b=PASSES, t=PACK),
         )
 
-        words = {}
+        words = []
 
         def gather_words(start, width):
             half, at = divmod(start, HALF)
-            cols = slice(start // 16, (start + width) // 16)
+            cols = slice(start // PER_COLUMN, (start + width) // PER_COLUMN)
             nc.vector.tensor_copy(words[half][:, 0, at : at + width], tab_w[:].indirect(box_list[:, cols]))
             nc.vector.tensor_copy(words[half][:, 1, at : at + width], tab_w[:].indirect(truck_list[:, cols]))
 
@@ -150,96 +160,89 @@ def tile_list_truck_box_appointment_kernel(
         def prepare_wc(b):
             raw = stage.tile([P, PACK, N], F32, name="wc_raw%d" % b, tag=("raw_b", "raw_a")[b])
             nc.sync.dma_start(out=raw[:], in_=wc[b * PASS : (b + 1) * PASS, :].rearrange("(p t) n -> p t n", t=PACK))
-            grouped = keep.tile([P, N * PACK], BF16, name="wc_grouped%d" % b, tag="wc_grouped%d" % b, align_bytes=64)
+            grouped = keep.tile([P, N * PACK], BF16, name="wc_grouped%d" % b, align_bytes=64)
             for n0 in range(0, N, P):
-                pool_cast(
+                gpsimd_cast(
                     grouped[:, n0 * PACK : (n0 + P) * PACK].rearrange("p (n t) -> p n t", t=PACK),
                     raw[:, :, n0 : n0 + P].rearrange("p t n -> p n t"),
                 )
             wc_q.append(quantise(grouped, N, "wc%d" % b))
 
-        sums = {}
-
-        def first_stage(start, width, b, summed):
+        def first_stage(start, width, b, summed=False, ring="unit", vector_reads=0):
             half, at = divmod(start, HALF)
             box_words = words[half][:, 0, at : at + width].bitcast(FP8X4)
             truck_words = words[half][:, 1, at : at + width].bitcast(FP8X4)
             gained = keep.tile([P, PACK, width], F32, name="gained%d_%d" % (start, b))
-            damp = keep.tile([P, PACK, width], F32, name="damp%d_%d" % (start, b), tag="damp%d_%d" % (start, b))
+            damp = keep.tile(
+                [P, PACK, width], F32, name="damp%d_%d" % (start, b), tag="damp%d_%d" % (start, b), align_bytes=64
+            )
             for t in range(PACK):
-                u = b * PACK + t
+                unit = b * PACK + t
                 if width == HALF:
-                    other = psum.tile([P, width], F32, name="other", tag="unit")[:]
-                    box = psum.tile([P, width], F32, name="box", tag="unit")[:]
+                    truck = psum.tile([P, width], F32, name="truck", tag=ring)[:]
+                    box = psum.tile([P, width], F32, name="box", tag=ring)[:]
                 else:
-                    bank = psum.tile([P, 2, width], F32, name="bank", tag="unit")
-                    other, box = bank[:, 0, :], bank[:, 1, :]
+                    bank = psum.tile([P, 2, width], F32, name="bank", tag=ring)
+                    truck, box = bank[:, 0, :], bank[:, 1, :]
                 cols = slice(t * P, (t + 1) * P)
 
-                def box_pass(place, stop):
+                def box_pass(target, stop):
                     nc.tensor.matmul_mx(
-                        out=place, lhsT=wa_q[b][0][:, cols].bitcast(FP8X4), lhsT_scale=wa_q[b][1][:, cols],
+                        out=target, lhsT=wa_q[b][0][:, cols].bitcast(FP8X4), lhsT_scale=wa_q[b][1][:, cols],
                         rhs=box_words, rhs_scale=box_scales[half][:, at : at + width], start=True, stop=stop,
                     )
 
                 box_pass(box, True)
                 if summed:
-                    box_pass(other, False)
+                    box_pass(truck, False)
                 nc.tensor.matmul_mx(
-                    out=other, lhsT=wb_w[:, 2 * u * P : 2 * (u + 1) * P].bitcast(FP4X4),
-                    lhsT_scale=wb_s[:, u * P : (u + 1) * P],
+                    out=truck, lhsT=wb_w[:, 2 * unit * P : 2 * (unit + 1) * P].bitcast(FP4X4),
+                    lhsT_scale=wb_s[:, unit * P : (unit + 1) * P],
                     rhs=truck_words, rhs_scale=truck_scales[half][:, at : at + width],
                     start=not summed, stop=True,
                 )
-                if (start, b, t) in EVAC_V:
+                if t >= PACK - vector_reads:
                     nc.vector.tensor_scalar(gained[:, t, :], box, gains[:, b, t : t + 1], None, ALU.mult)
                 else:
                     nc.scalar.activation(gained[:, t, :], box, ACT.Copy, scale=gains[:, b, t : t + 1])
                 if summed:
-                    nc.scalar.activation(damp[:, t, :], other, ACT.Abs)
+                    nc.scalar.activation(damp[:, t, :], truck, ACT.Abs)
                 else:
                     nc.vector.scalar_tensor_tensor(
-                        damp[:, t, :], gained[:, t, :], inv_gains[:, b, t : t + 1], other, ALU.mult, ALU.add
+                        damp[:, t, :], gained[:, t, :], inv_gains[:, b, t : t + 1], truck, ALU.mult, ALU.add
                     )
-            return start, b, gained, damp, summed
+            return gained[:], damp[:]
 
         h_q = {}
         for half in range(S // HALF):
             for b in range(PASSES):
+                codes_name, scales_name = "h_codes%d_%d" % (half, b), "h_scales%d_%d" % (half, b)
                 h_q[half, b] = (
-                    keep.tile([P, HALF], U32, name="h_codes%d_%d" % (half, b), tag="h_codes%d_%d" % (half, b), align_bytes=64),
-                    keep.tile([P, HALF], U8, name="h_scales%d_%d" % (half, b), tag="h_scales%d_%d" % (half, b), align_bytes=64),
+                    keep.tile([P, HALF], U32, name=codes_name, tag=codes_name, align_bytes=64),
+                    keep.tile([P, HALF], U8, name=scales_name, tag=scales_name, align_bytes=64),
                 )
 
-        def damping(sums, skip, width, pool=work, tag="h"):
-            start, b, gained, damp, summed = sums
-            gained, damp = gained[:, :, skip : skip + width], damp[:, :, skip : skip + width]
-            if not summed:
-                nc.scalar.activation(damp, damp, ACT.Abs)
-            nc.scalar.activation(damp, damp, ACT.Abs_reciprocal_sqrt, bias=1.0)
-            nc.scalar.activation(damp, damp, ACT.Square)
+        def make_h(start, b, gained, size, pool=work, tag="h"):
+            width = size.shape[2]
+            nc.scalar.activation(size, size, ACT.Abs_reciprocal_sqrt, bias=1.0)
+            nc.scalar.activation(size, size, ACT.Square)
             h = pool.tile([P, width * PACK], BF16, name="h", tag=tag, align_bytes=64)
             nc.vector.tensor_tensor(
-                h[:].rearrange("p (c i t) -> p c t i", i=4, t=PACK),
-                gained.rearrange("p t (c i) -> p c t i", i=4),
-                damp.rearrange("p t (c i) -> p c t i", i=4),
+                h[:].rearrange("p (c i t) -> p c t i", i=LINE, t=PACK),
+                gained.rearrange("p t (c i) -> p c t i", i=LINE),
+                size.rearrange("p t (c i) -> p c t i", i=LINE),
                 ALU.mult,
             )
-            half, at = divmod(start + skip, HALF)
+            half, at = divmod(start, HALF)
             codes, scales = h_q[half, b]
             nc.vector.quantize_mx(
                 out=codes[:, at : at + width].bitcast(FP8X4), scales=scales[:, at : at + width], in_=h[:]
             )
 
-        def place(half, q, y):
-            offsets = slot_list[:, half * HALF // 16 : (half + 1) * HALF // 16]
-            cols = slice(half * HALF, (half + 1) * HALF)
-            nc.vector.tensor_tensor(pages[q][:].indirect(offsets), y[:], factors[:, cols], ALU.mult)
-
         def second_stage(half):
-            accs = [psum.tile([P, HALF], F32, name="acc%d" % q, tag="acc") for q in range(N // P)]
+            accs = [psum.tile([P, HALF], F32, name="acc%d" % q, tag="acc") for q in range(PAGES)]
             for b in range(PASSES):
-                for q in range(N // P):
+                for q in range(PAGES):
                     rows = slice(q * P, (q + 1) * P)
                     nc.tensor.matmul_mx(
                         out=accs[q][:], lhsT=wc_q[b][0][:, rows].bitcast(FP8X4), lhsT_scale=wc_q[b][1][:, rows],
@@ -247,42 +250,58 @@ def tile_list_truck_box_appointment_kernel(
                         start=(b == 0), stop=(b == PASSES - 1),
                     )
             ys = []
-            for q in range(N // P):
-                ys.append(work.tile([P, HALF], F32, name="y", tag="y", bufs=8))
+            for q in range(PAGES):
+                ys.append(work.tile([P, HALF], F32, name="y", tag="y", bufs=PAGES * S // HALF))
                 nc.scalar.activation(ys[q][:], accs[q][:], ACT.Tanh)
             return ys
 
-        words[0] = keep.tile([P, 2, HALF], U32, name="words0", align_bytes=64)
-        gather_words(0, 256)
-        a0 = first_stage(0, 256, 0, True)
-        gather_words(256, 256)
-        a1 = first_stage(256, 256, 0, False)
-        wa_q[1] = quantise(group_wa(1, pool_group_wa), PASS, "wa1")
-        damping(a0, 0, 256)
-        a2 = first_stage(0, 512, 1, False)
-        damping(a1, 0, 256)
-        prepare_wc(0)
-        prepare_wc(1)
+        def place(half, q, y):
+            offsets = slot_list[:, half * HALF // PER_COLUMN : (half + 1) * HALF // PER_COLUMN]
+            cols = slice(half * HALF, (half + 1) * HALF)
+            nc.vector.tensor_tensor(pages[q][:].indirect(offsets), y[:], factors[:, cols], ALU.mult)
+
+        words.append(keep.tile([P, 2, HALF], U32, name="words0", align_bytes=64))
+        gather_words(0, STRIP)
+        gained_00, size_00 = first_stage(0, STRIP, 0, summed=True)
+        gather_words(STRIP, STRIP)
+        gained_10, damp_10 = first_stage(STRIP, STRIP, 0)
+        wa_q.append(quantise(group_wa(1, gpsimd_cast_by_t), PASS, "wa1"))
+        make_h(0, 0, gained_00, size_00)
+        gained_first, damp_first = first_stage(0, HALF, 1)
+        nc.scalar.activation(damp_10, damp_10, ACT.Abs)
+        make_h(STRIP, 0, gained_10, damp_10)
+        for b in range(PASSES):
+            prepare_wc(b)
         factors = stage.tile([P, S], F32, name="factors", tag="raw_b")
         nc.sync.dma_start(out=factors[:], in_=wgo)
-        truck_scales.append(gather_scales(truck_list, 1, "truck", "wc_grouped0"))
-        words[1] = keep.tile([P, 2, HALF], U32, name="words1", tag="wa_grouped1", align_bytes=64)
-        gather_words(512, 512)
-        damping(a2, 0, 256)
-        b0 = first_stage(512, 512, 0, False)
-        damping(a2, 256, 256, keep, "h_last")
-        b1 = first_stage(512, 256, 1, False)
+
+        words.append(keep.tile([P, 2, HALF], U32, name="words1", tag="wa_grouped1", align_bytes=64))
+        gather_words(HALF, HALF)
+        early, late = slice(0, STRIP), slice(STRIP, HALF)
+        nc.scalar.activation(damp_first[:, :, early], damp_first[:, :, early], ACT.Abs)
+        make_h(0, 1, gained_first[:, :, early], damp_first[:, :, early])
+        gained_second, damp_second = first_stage(HALF, HALF, 0, vector_reads=BOX_READS_ON_VECTOR)
+        nc.scalar.activation(damp_first[:, :, late], damp_first[:, :, late], ACT.Abs)
+        make_h(STRIP, 1, gained_first[:, :, late], damp_first[:, :, late], keep, "h_last")
+        gained_21, damp_21 = first_stage(HALF, STRIP, 1)
+
         ys = second_stage(0)
-        for q, tag in enumerate(("h_last", "h_codes0_1", "h_scales0_1")):
-            pages.append(keep.tile([P, T2], F32, name="page%d" % (q + 1), tag=tag, align_bytes=64))
-            nc.gpsimd.memset(pages[q + 1][:], 0.0)
-        for q in range(4):
+        clear_page("h_last")
+        clear_page("h_codes0_1")
+        for q in range(PAGES - 1):
             place(0, q, ys[q])
-        damping(b0, 0, 512)
-        b2 = first_stage(768, 256, 1, True)
-        damping(b1, 0, 256)
-        damping(b2, 0, 256)
+        size_second = keep.tile([P, PACK, HALF], F32, name="size_second", tag="h_scales0_1", align_bytes=64)[:]
+        nc.scalar.activation(size_second, damp_second, ACT.Abs)
+        make_h(HALF, 0, gained_second, size_second)
+        clear_page("damp%d_0" % HALF)
+        place(0, PAGES - 1, ys[PAGES - 1])
+
+        gained_31, size_31 = first_stage(HALF + STRIP, STRIP, 1, summed=True, ring="acc")
+        nc.vector.scalar_tensor_tensor(damp_21, damp_21, -1.0, damp_21, ALU.mult, ALU.max)
+        make_h(HALF, 1, gained_21, damp_21)
+        make_h(HALF + STRIP, 1, gained_31, size_31)
+
         ys = second_stage(1)
-        for q in range(4):
+        for q in range(PAGES):
             place(1, q, ys[q])
             nc.sync.dma_start(out=out[q * P : (q + 1) * P, :], in_=pages[q][:])

from contextlib import ExitStack

import concourse.mybir as mybir

K, T, S, H, N, T2 = 512, 4096, 1024, 1024, 512, 2048
FLOPS = 2 * K * H * S * 2 + 2 * H * N * S

F32 = mybir.dt.float32
BF16 = mybir.dt.bfloat16
I32 = mybir.dt.int32
U32 = mybir.dt.uint32
U16 = mybir.dt.uint16
U8 = mybir.dt.uint8
FP8X4 = mybir.dt.float8_e4m3fn_x4
FP4X4 = mybir.dt.float4_e2m1fn_x4
ACT = mybir.ActivationFunctionType
ALU = mybir.AluOpType

P = 128
PACK = 4
PASS = P * PACK
PASSES = H // PASS
QUADRANTS = 4
PER_COLUMN = 16
HALF = S // 2
STRIP = HALF // 2
PAGES = N // P
LINE = 4
ACC_BANKS = PAGES
BOX_READS_ON_VECTOR = 3


def tile_list_truck_box_appointment_kernel(
    tc, tab_words, tab_scales, offs, offs2, offs3, wa, wb_words, wb_scales, gain, wc, wgo, out
):
    nc = tc.nc
    with ExitStack() as ctx:
        lists = ctx.enter_context(tc.tile_pool(name="lists", bufs=1))
        keep = ctx.enter_context(tc.tile_pool(name="keep", bufs=1))
        stage = ctx.enter_context(tc.tile_pool(name="stage", bufs=1))
        work = ctx.enter_context(tc.tile_pool(name="work", bufs=3))
        psum = ctx.enter_context(tc.psum_pool(name="psum", bufs=ACC_BANKS))

        tab_s = keep.tile([P, T], U8, name="tab_s", align_bytes=64)
        nc.vector.memset(tab_s[:].bitcast(I32), 0)
        wb_s_raw = keep.tile([P, H], U8, name="wb_s_raw", align_bytes=64)
        nc.vector.memset(wb_s_raw[:].bitcast(I32), 0)

        box_list = lists.tile([P, S // PER_COLUMN], U16, name="box_list")
        truck_list = lists.tile([P, S // PER_COLUMN], U16, name="truck_list")
        slot_list = lists.tile([P, S // PER_COLUMN], U16, name="slot_list")
        gains = keep.tile([P, PASSES, PACK], F32, name="gains")
        nc.scalar.dma_start(out=gains[:], in_=gain.rearrange("(b p t) -> p b t", b=PASSES, t=PACK))
        nc.sync.dma_start(box_list[:], offs)
        nc.sync.dma_start(truck_list[:], offs2)
        nc.sync.dma_start(slot_list[:], offs3)
        for q in range(QUADRANTS):
            nc.sync.dma_start(
                out=tab_s[32 * q : 32 * q + 4, :].bitcast(I32), in_=tab_scales[0, 4 * q : 4 * q + 4, :].bitcast(I32)
            )
        for q in range(QUADRANTS):
            nc.gpsimd.dma_start(
                out=wb_s_raw[32 * q : 32 * q + 4, :].bitcast(I32), in_=wb_scales[0, 4 * q : 4 * q + 4, :].bitcast(I32)
            )

        wa_rows = wa.rearrange("(p j) c -> p j c", j=PACK)

        def load_wa(b):
            raw = stage.tile([P, PACK, PASS], F32, name="wa_raw%d" % b, tag="raw_a")
            nc.sync.dma_start(out=raw[:], in_=wa_rows[:, :, b * PASS : (b + 1) * PASS])
            return raw

        wa_raw = [load_wa(0)]
        wb_raw = stage.tile([P, 2 * H], U8, name="wb_raw", tag="raw_b")
        nc.sync.dma_start(out=wb_raw[:].bitcast(I32), in_=wb_words[0].bitcast(I32))
        tab_w = keep.tile([P, T], U32, name="tab_w", align_bytes=64)
        nc.sync.dma_start(out=tab_w[:].bitcast(I32), in_=tab_words[0].rearrange("p t i -> p (t i)").bitcast(I32))

        nonzero = keep.tile([P, PASSES, PACK], F32, name="nonzero")
        nc.vector.scalar_tensor_tensor(nonzero[:], gains[:], 0.0, gains[:], ALU.is_equal, ALU.add)
        inv_size = keep.tile([P, PASSES, PACK], F32, name="inv_size")
        nc.scalar.activation(inv_size[:], nonzero[:], ACT.Abs_reciprocal_sqrt)
        nc.scalar.activation(inv_size[:], inv_size[:], ACT.Square)
        signs = keep.tile([P, PASSES, PACK], F32, name="signs")
        nc.scalar.activation(signs[:], nonzero[:], ACT.Sign)
        guess = keep.tile([P, PASSES, PACK], F32, name="guess")
        nc.vector.tensor_tensor(guess[:], inv_size[:], signs[:], ALU.mult)
        polish = keep.tile([P, PASSES, PACK], F32, name="polish")
        nc.vector.tensor_tensor(polish[:], guess[:], nonzero[:], ALU.mult)
        nc.vector.tensor_scalar(polish[:], polish[:], -1.0, 2.0, ALU.mult, ALU.add)
        inv_gains = keep.tile([P, PASSES, PACK], F32, name="inv_gains")
        nc.vector.tensor_tensor(inv_gains[:], guess[:], polish[:], ALU.mult)

        pages = [keep.tile([P, T2], F32, name="page0")]
        nc.vector.memset(pages[0][:].bitcast(I32), 0)

        def clear_page(tag):
            page = keep.tile([P, T2], F32, name="page%d" % len(pages), tag=tag, align_bytes=64)
            nc.gpsimd.memset(page[:], 0.0)
            pages.append(page)

        def quantise(grouped, width, name):
            codes = keep.tile([P, width], U32, name=name + "_codes", align_bytes=64)
            scales = keep.tile([P, width], U8, name=name + "_scales", align_bytes=64)
            nc.vector.quantize_mx(out=codes[:].bitcast(FP8X4), scales=scales[:], in_=grouped[:])
            return codes, scales

        def group_wa(b, cast):
            grouped = keep.tile([P, PASS * PACK], BF16, name="wa_grouped%d" % b, tag="wa_grouped%d" % b, align_bytes=64)
            cast(
                grouped[:].rearrange("p (t m j) -> p m t j", t=PACK, j=PACK),
                wa_raw[b][:].rearrange("p j (m t) -> p m t j", t=PACK),
            )
            return grouped

        def gpsimd_cast(dst, src):
            nc.gpsimd.tensor_scalar(dst, src, 1.0, 0.0, ALU.mult, ALU.add)

        def gpsimd_cast_by_t(dst, src):
            for t in range(PACK):
                gpsimd_cast(dst[:, :, t, :], src[:, :, t, :])

        wa_grouped = group_wa(0, nc.scalar.copy)
        wa_raw.append(load_wa(1))

        wb_w = keep.tile([P, 2 * H], U8, name="wb_w", align_bytes=64)
        nc.scalar.copy(
            wb_w[:].bitcast(U16).rearrange("p (b t m) -> p b t m", b=PASSES, t=PACK),
            wb_raw[:].bitcast(U16).rearrange("p (b m t) -> p b t m", b=PASSES, t=PACK),
        )

        def gather_scales(offsets, half, name):
            picked = keep.tile([P, HALF], U8, name="%s_scales%d" % (name, half), align_bytes=64)
            cols = HALF // PER_COLUMN
            nc.vector.tensor_copy(picked[:], tab_s[:].indirect(offsets[:, half * cols : (half + 1) * cols]))
            return picked

        box_scales = [gather_scales(box_list, 0, "box")]
        truck_scales = [gather_scales(truck_list, 0, "truck")]
        wa_q = [quantise(wa_grouped, PASS, "wa0")]
        box_scales.append(gather_scales(box_list, 1, "box"))
        truck_scales.append(gather_scales(truck_list, 1, "truck"))

        wb_s = keep.tile([P, H], U8, name="wb_s", tag="wa_grouped0", align_bytes=64)
        nc.vector.tensor_copy(
            wb_s[:].rearrange("p (b t m) -> p b t m", b=PASSES, t=PACK),
            wb_s_raw[:].rearrange("p (b m t) -> p b t m", b=PASSES, t=PACK),
        )

        words = []

        def gather_words(start, width):
            half, at = divmod(start, HALF)
            cols = slice(start // PER_COLUMN, (start + width) // PER_COLUMN)
            nc.vector.tensor_copy(words[half][:, 0, at : at + width], tab_w[:].indirect(box_list[:, cols]))
            nc.vector.tensor_copy(words[half][:, 1, at : at + width], tab_w[:].indirect(truck_list[:, cols]))

        wc_q = []

        def prepare_wc(b):
            raw = stage.tile([P, PACK, N], F32, name="wc_raw%d" % b, tag=("raw_b", "raw_a")[b])
            nc.sync.dma_start(out=raw[:], in_=wc[b * PASS : (b + 1) * PASS, :].rearrange("(p t) n -> p t n", t=PACK))
            grouped = keep.tile([P, N * PACK], BF16, name="wc_grouped%d" % b, align_bytes=64)
            for n0 in range(0, N, P):
                gpsimd_cast(
                    grouped[:, n0 * PACK : (n0 + P) * PACK].rearrange("p (n t) -> p n t", t=PACK),
                    raw[:, :, n0 : n0 + P].rearrange("p t n -> p n t"),
                )
            wc_q.append(quantise(grouped, N, "wc%d" % b))

        def first_stage(start, width, b, summed=False, ring="unit", vector_reads=0):
            half, at = divmod(start, HALF)
            box_words = words[half][:, 0, at : at + width].bitcast(FP8X4)
            truck_words = words[half][:, 1, at : at + width].bitcast(FP8X4)
            gained = keep.tile([P, PACK, width], F32, name="gained%d_%d" % (start, b))
            damp = keep.tile(
                [P, PACK, width], F32, name="damp%d_%d" % (start, b), tag="damp%d_%d" % (start, b), align_bytes=64
            )
            for t in range(PACK):
                unit = b * PACK + t
                if width == HALF:
                    truck = psum.tile([P, width], F32, name="truck", tag=ring)[:]
                    box = psum.tile([P, width], F32, name="box", tag=ring)[:]
                else:
                    bank = psum.tile([P, 2, width], F32, name="bank", tag=ring)
                    truck, box = bank[:, 0, :], bank[:, 1, :]
                cols = slice(t * P, (t + 1) * P)

                def box_pass(target, stop):
                    nc.tensor.matmul_mx(
                        out=target, lhsT=wa_q[b][0][:, cols].bitcast(FP8X4), lhsT_scale=wa_q[b][1][:, cols],
                        rhs=box_words, rhs_scale=box_scales[half][:, at : at + width], start=True, stop=stop,
                    )

                box_pass(box, True)
                if summed:
                    box_pass(truck, False)
                nc.tensor.matmul_mx(
                    out=truck, lhsT=wb_w[:, 2 * unit * P : 2 * (unit + 1) * P].bitcast(FP4X4),
                    lhsT_scale=wb_s[:, unit * P : (unit + 1) * P],
                    rhs=truck_words, rhs_scale=truck_scales[half][:, at : at + width],
                    start=not summed, stop=True,
                )
                if t >= PACK - vector_reads:
                    nc.vector.tensor_scalar(gained[:, t, :], box, gains[:, b, t : t + 1], None, ALU.mult)
                else:
                    nc.scalar.activation(gained[:, t, :], box, ACT.Copy, scale=gains[:, b, t : t + 1])
                if summed:
                    nc.scalar.activation(damp[:, t, :], truck, ACT.Abs)
                else:
                    nc.vector.scalar_tensor_tensor(
                        damp[:, t, :], gained[:, t, :], inv_gains[:, b, t : t + 1], truck, ALU.mult, ALU.add
                    )
            return gained[:], damp[:]

        h_q = {}
        for half in range(S // HALF):
            for b in range(PASSES):
                codes_name, scales_name = "h_codes%d_%d" % (half, b), "h_scales%d_%d" % (half, b)
                h_q[half, b] = (
                    keep.tile([P, HALF], U32, name=codes_name, tag=codes_name, align_bytes=64),
                    keep.tile([P, HALF], U8, name=scales_name, tag=scales_name, align_bytes=64),
                )

        def make_h(start, b, gained, size, pool=work, tag="h"):
            width = size.shape[2]
            nc.scalar.activation(size, size, ACT.Abs_reciprocal_sqrt, bias=1.0)
            nc.scalar.activation(size, size, ACT.Square)
            h = pool.tile([P, width * PACK], BF16, name="h", tag=tag, align_bytes=64)
            nc.vector.tensor_tensor(
                h[:].rearrange("p (c i t) -> p c t i", i=LINE, t=PACK),
                gained.rearrange("p t (c i) -> p c t i", i=LINE),
                size.rearrange("p t (c i) -> p c t i", i=LINE),
                ALU.mult,
            )
            half, at = divmod(start, HALF)
            codes, scales = h_q[half, b]
            nc.vector.quantize_mx(
                out=codes[:, at : at + width].bitcast(FP8X4), scales=scales[:, at : at + width], in_=h[:]
            )

        def second_stage(half):
            accs = [psum.tile([P, HALF], F32, name="acc%d" % q, tag="acc") for q in range(PAGES)]
            for b in range(PASSES):
                for q in range(PAGES):
                    rows = slice(q * P, (q + 1) * P)
                    nc.tensor.matmul_mx(
                        out=accs[q][:], lhsT=wc_q[b][0][:, rows].bitcast(FP8X4), lhsT_scale=wc_q[b][1][:, rows],
                        rhs=h_q[half, b][0][:].bitcast(FP8X4), rhs_scale=h_q[half, b][1][:],
                        start=(b == 0), stop=(b == PASSES - 1),
                    )
            ys = []
            for q in range(PAGES):
                ys.append(work.tile([P, HALF], F32, name="y", tag="y", bufs=PAGES * S // HALF))
                nc.scalar.activation(ys[q][:], accs[q][:], ACT.Tanh)
            return ys

        def place(half, q, y):
            offsets = slot_list[:, half * HALF // PER_COLUMN : (half + 1) * HALF // PER_COLUMN]
            cols = slice(half * HALF, (half + 1) * HALF)
            nc.vector.tensor_tensor(pages[q][:].indirect(offsets), y[:], factors[:, cols], ALU.mult)

        words.append(keep.tile([P, 2, HALF], U32, name="words0", align_bytes=64))
        gather_words(0, STRIP)
        gained_00, size_00 = first_stage(0, STRIP, 0, summed=True)
        gather_words(STRIP, STRIP)
        gained_10, damp_10 = first_stage(STRIP, STRIP, 0)
        wa_q.append(quantise(group_wa(1, gpsimd_cast_by_t), PASS, "wa1"))
        make_h(0, 0, gained_00, size_00)
        gained_first, damp_first = first_stage(0, HALF, 1)
        nc.scalar.activation(damp_10, damp_10, ACT.Abs)
        make_h(STRIP, 0, gained_10, damp_10)
        for b in range(PASSES):
            prepare_wc(b)
        factors = stage.tile([P, S], F32, name="factors", tag="raw_b")
        nc.sync.dma_start(out=factors[:], in_=wgo)

        words.append(keep.tile([P, 2, HALF], U32, name="words1", tag="wa_grouped1", align_bytes=64))
        gather_words(HALF, HALF)
        early, late = slice(0, STRIP), slice(STRIP, HALF)
        nc.scalar.activation(damp_first[:, :, early], damp_first[:, :, early], ACT.Abs)
        make_h(0, 1, gained_first[:, :, early], damp_first[:, :, early])
        gained_second, damp_second = first_stage(HALF, HALF, 0, vector_reads=BOX_READS_ON_VECTOR)
        nc.scalar.activation(damp_first[:, :, late], damp_first[:, :, late], ACT.Abs)
        make_h(STRIP, 1, gained_first[:, :, late], damp_first[:, :, late], keep, "h_last")
        gained_21, damp_21 = first_stage(HALF, STRIP, 1)

        ys = second_stage(0)
        clear_page("h_last")
        clear_page("h_codes0_1")
        for q in range(PAGES - 1):
            place(0, q, ys[q])
        size_second = keep.tile([P, PACK, HALF], F32, name="size_second", tag="h_scales0_1", align_bytes=64)[:]
        nc.scalar.activation(size_second, damp_second, ACT.Abs)
        make_h(HALF, 0, gained_second, size_second)
        clear_page("damp%d_0" % HALF)
        place(0, PAGES - 1, ys[PAGES - 1])

        gained_31, size_31 = first_stage(HALF + STRIP, STRIP, 1, summed=True, ring="acc")
        nc.vector.scalar_tensor_tensor(damp_21, damp_21, -1.0, damp_21, ALU.mult, ALU.max)
        make_h(HALF, 1, gained_21, damp_21)
        make_h(HALF + STRIP, 1, gained_31, size_31)

        ys = second_stage(1)
        for q in range(PAGES):
            place(1, q, ys[q])
            nc.sync.dma_start(out=out[q * P : (q + 1) * P, :], in_=pages[q][:])
